import numpy as np
import ml_dtypes


def mxq(x, axis, fmt="e4m3"):
    dtype, down = {"e4m3": (ml_dtypes.float8_e4m3fn, 7), "e5m2": (ml_dtypes.float8_e5m2, 14)}[fmt]
    v = np.moveaxis(np.asarray(x, np.float32).astype(ml_dtypes.bfloat16).astype(np.float64), axis, -1)
    blocks = v.reshape(v.shape[:-1] + (-1, 32))
    amax = np.abs(blocks).max(-1, keepdims=True)
    byte = np.maximum(np.where(amax > 0, np.frexp(amax)[1] - 1 + 127, 0) - down, 1)
    scale = np.exp2(byte - 127.0)
    codes = (blocks / scale).astype(np.float32).astype(dtype).astype(np.float64)
    return np.moveaxis((codes * scale).reshape(v.shape), -1, axis)


WIDE = False


def mx_kscale(k):
    if not WIDE:
        return np.ones(k)
    levels = np.array([10, -10, 5, -5, 0])
    if k % 512:
        return np.exp2(np.random.permutation(np.resize(levels, k // 32))).repeat(32)
    a = np.empty((k // 512, 16))
    for p in range(k // 512):
        a[p, :8] = np.random.permutation(np.resize(levels, 8))
        for g in range(8):
            far = levels[np.abs(levels - a[p, g]) >= 10]
            a[p, g + 8] = far[np.random.randint(len(far))]
    return np.exp2(a.ravel()).repeat(32)


def f64(x):
    return np.asarray(x).astype(np.float64)


def striped(idx):
    return np.tile(np.asarray(idx).reshape(-1, 16).T, (8, 1)).astype(np.uint16)


def unstriped(offs):
    return offs[:16].T.reshape(-1).astype(np.int64)


E2M1 = np.array([0.0, 0.5, 1.0, 1.5, 2.0, 3.0, 4.0, 6.0, -0.0, -0.5, -1.0, -1.5, -2.0, -3.0, -4.0, -6.0])


def pack_weight(w, fmt):
    k, n = w.shape
    w = f64(np.asarray(w, np.float32).astype(ml_dtypes.bfloat16)).reshape(k // 32, 32, n)
    amax = np.abs(w).max(1)
    if fmt == "e4m3":
        byte = np.frexp(amax)[1] - 1 + 127 - 7
    else:
        mant, ex = np.frexp(amax / 6.0)
        byte = np.where(mant > 0.5, ex, ex - 1) + 127
    byte = np.clip(np.where(amax > 0, byte, 1), 1, 254)
    scaled = (w * np.exp2(127.0 - byte)[:, None, :]).reshape(k, n).astype(np.float32)
    by_word = np.ascontiguousarray(scaled.reshape(k // 512, 128, 4, n).transpose(0, 1, 3, 2))
    if fmt == "e4m3":
        words = by_word.astype(ml_dtypes.float8_e4m3fn).view(np.uint8)
    else:
        c = by_word.astype(ml_dtypes.float4_e2m1fn).view(np.uint8) & 0xF
        words = (c[..., 0::2] | (c[..., 1::2] << 4)).reshape(k // 512, 128, 2 * n)
    return np.ascontiguousarray(words), np.ascontiguousarray(byte.astype(np.uint8).reshape(k // 512, 16, n))


def unpack_weight(words, scales, fmt):
    g, _, n = scales.shape
    words = np.ascontiguousarray(words).reshape(g, 128, n, -1)
    if fmt == "e4m3":
        vals = words.view(ml_dtypes.float8_e4m3fn).astype(np.float64)
    else:
        nib = np.empty((g, 128, n, 4), np.uint8)
        nib[..., 0::2] = words & 0xF
        nib[..., 1::2] = words >> 4
        vals = E2M1[nib]
    vals = vals * np.repeat(np.exp2(scales.astype(np.float64) - 127.0), 8, axis=1)[..., None]
    return vals.transpose(0, 1, 3, 2).reshape(g * 512, n)


D, T, I, Q, E, G, M = 512, 2048, 512, 256, 512, 64, 1024


def setup_inputs():
    n = np.random.standard_normal
    idx = np.random.permutation(T)[:I]
    idx2 = np.random.permutation(T)[:I]
    idx3 = np.random.permutation(M)[:Q]
    fd = mx_kscale(D)
    fi = mx_kscale(I)
    ti = np.ones(T)
    ti[idx] = fi
    keysp = pack_weight(n((D, T)) / fd[:, None], "e4m3")
    return {
        "query": (n((D, Q)) * 1.0 / np.sqrt(D) * fd[:, None]).astype(np.float32),
        "query2": (n((D, Q)) * 1.0 / np.sqrt(D) * fd[:, None]).astype(np.float32),
        "keys_words": keysp[0],
        "keys_scales": keysp[1],
        "lam": (np.random.uniform(1.0, 3.0, (Q, 1))).astype(np.float32),
        "os": (np.random.uniform(4.0, 16.0, (1, I)) * fi).astype(np.float32),
        "vals": (n((E, T)) / ti).astype(np.float32),
        "member": (n((E, M))).astype(np.float32),
        "mgain": np.tile(np.random.uniform(0.5, 2.0, M), (128, 1)).astype(np.float32),
        "offs": striped(idx),
        "offs2": striped(idx2),
        "offs3": striped(idx3),
    }


def reference(query, query2, keys_words, keys_scales, lam, os, vals, member, mgain, offs, offs2, offs3):
    idx = unstriped(offs)
    idx2 = unstriped(offs2)
    idx3 = unstriped(offs3)
    keysu = unpack_weight(keys_words, keys_scales, "e4m3")
    queryq = mxq(f64(query), 0, "e4m3")
    a = queryq.T @ keysu
    query2q = mxq(f64(query2), 0, "e4m3")
    b = query2q.T @ keysu
    la = np.square(a[:, idx]) + np.square(b[:, idx])
    lb = np.square(a[:, idx2]) + np.square(b[:, idx2])
    s = (a[:, idx] * a[:, idx2] + b[:, idx] * b[:, idx2]) / np.sqrt(la * lb + 0.5) * f64(lam)
    p = np.exp(s)
    pg = p.reshape(Q, G, I // G).sum(axis=2)
    z0 = np.sum(pg, axis=1, keepdims=True)
    k0 = 1.0 / (z0 - pg)
    kr = np.repeat(k0, I // G, axis=1)
    w = p * kr
    wo1 = w * f64(os)
    wt1 = wo1.T
    vt1 = f64(vals)[:, idx].T
    vt1q = mxq(vt1, 0, "e4m3")
    wt1q = mxq(wt1, 0, "e4m3")
    o = vt1q.T @ wt1q
    y = o * f64(mgain)[:1][:, idx3] + f64(member)[:, idx3]
    return y

@@ -1,0 +1,336 @@
+from contextlib import ExitStack
+
+import concourse.mybir as mybir
+from concourse.masks import make_identity
+
+D, T, I, Q, E, G, M = 512, 2048, 512, 256, 512, 64, 1024
+FLOPS = 2 * (2 * Q * D * T + E * I * Q)
+
+F32 = mybir.dt.float32
+BF16 = mybir.dt.bfloat16
+I32 = mybir.dt.int32
+U32 = mybir.dt.uint32
+U16 = mybir.dt.uint16
+U8 = mybir.dt.uint8
+FP8X4 = mybir.dt.float8_e4m3fn_x4
+ACT = mybir.ActivationFunctionType
+ALU = mybir.AluOpType
+AXIS = mybir.AxisListType
+
+P = 128
+PACK = 4
+BANK = 512
+BANKS = 8
+Q_TILES = Q // P
+E_TILES = E // P
+KEY_CHUNKS = T // BANK
+HALF = I // 2
+
+
+def tile_attend_planecos_outside_bymember_kernel(
+    tc, query, query2, keys_words, keys_scales, lam, slot_factor, vals, member, mgain, offs, offs2, offs3, out
+):
+    nc = tc.nc
+    with ExitStack() as ctx:
+        held = ctx.enter_context(tc.tile_pool(name="held", bufs=1))
+        work = ctx.enter_context(tc.tile_pool(name="work", bufs=2))
+        psum = ctx.enter_context(tc.psum_pool(name="psum", bufs=1))
+
+        def bank(n):
+            return psum.tile([P, BANK], F32, name=f"bank{n}", tag=f"bank{n}")
+
+        def vector_copy(dst, src):
+            nc.vector.tensor_copy(out=dst, in_=src)
+
+        def scalar_copy(dst, src):
+            nc.scalar.copy(out=dst, in_=src)
+
+        def scalar_move(dst, src):
+            nc.scalar.activation(out=dst, in_=src, func=ACT.Copy)
+
+        key_scales = held.tile([P, T], U8, name="key_scales", align_bytes=64)
+        nc.gpsimd.memset(key_scales[:].bitcast(U32), 0)
+        for quad in range(4):
+            nc.sync.dma_start(
+                out=key_scales[32 * quad : 32 * quad + 4, :].bitcast(I32),
+                in_=keys_scales[0, 4 * quad : 4 * quad + 4, :].bitcast(I32),
+            )
+        words_hbm = keys_words[0].rearrange("p n t -> p (n t)").bitcast(I32)
+        raw_q = [
+            [held.tile([P, PACK, P], F32, name=f"raw_q{k}_{t}") for t in range(Q_TILES)] for k in range(2)
+        ]
+        key_words = [held.tile([P, T // 2], U32, name=f"key_words{n}", align_bytes=64) for n in range(2)]
+
+        def load_query(k, t):
+            rows = (query, query2)[k].rearrange("(p j) w -> p j w", j=PACK)
+            nc.sync.dma_start(out=raw_q[k][t][:], in_=rows[:, :, t * P : (t + 1) * P])
+
+        load_query(0, 0)
+        for n in range(2):
+            nc.sync.dma_start(out=key_words[n][:].bitcast(I32), in_=words_hbm[:, n * T // 2 : (n + 1) * T // 2])
+        load_query(1, 0)
+        list1 = held.tile([P, I // 16], U16, name="list1")
+        list2 = held.tile([P, I // 16], U16, name="list2")
+        list3 = held.tile([P, Q // 16], U16, name="list3")
+        nc.sync.dma_start(list1[:], offs)
+        nc.sync.dma_start(list2[:], offs2)
+        load_query(0, 1)
+        load_query(1, 1)
+        vals_sb = [held.tile([P, T], F32, name=f"vals{c}") for c in range(E_TILES)]
+        for c in range(E_TILES):
+            nc.sync.dma_start(out=vals_sb[c][:], in_=vals[c * P : (c + 1) * P, :])
+        nc.sync.dma_start(list3[:], offs3)
+        mgain_sb = held.tile([P, M], F32, name="mgain_sb")
+        nc.sync.dma_start(out=mgain_sb[:], in_=mgain)
+        member_sb = [held.tile([P, M], F32, name=f"member{c}") for c in range(E_TILES)]
+        for c in range(E_TILES):
+            nc.sync.dma_start(out=member_sb[c][:], in_=member[c * P : (c + 1) * P, :])
+
+        ident = held.tile([P, P], F32, name="ident")
+        make_identity(nc, ident[:])
+        half_col = held.tile([P, 1], F32, name="half_col", tag="half_col")
+        nc.gpsimd.memset(half_col[:], 0.5)
+        lam_sb = [held.tile([P, 1], F32, name=f"lam{t}", tag=f"lam{t}") for t in range(Q_TILES)]
+        for t in range(Q_TILES):
+            nc.gpsimd.dma_start(out=lam_sb[t][:], in_=lam[t * P : (t + 1) * P, :])
+        os_sb = held.tile([P, PACK], F32, name="os_sb")
+        nc.gpsimd.dma_start(out=os_sb[:], in_=slot_factor.rearrange("o (p j) -> (o p) j", j=PACK))
+
+        def quantise_query(k, t):
+            woven = held.tile([P, P, PACK], BF16, name=f"q_woven{k}_{t}", align_bytes=64)
+            vector_copy(
+                woven[:].rearrange("p (c i) j -> p c j i", i=4),
+                raw_q[k][t][:].rearrange("p j (c i) -> p c j i", i=4),
+            )
+            words = held.tile([P, P], U32, name=f"q_words{k}_{t}", align_bytes=64)
+            scales = held.tile([P, P], U8, name=f"q_scales{k}_{t}", align_bytes=64)
+            nc.vector.quantize_mx(
+                out=words[:].bitcast(FP8X4), scales=scales[:], in_=woven[:].rearrange("p w j -> p (w j)")
+            )
+            return words, scales
+
+        quantised = {}
+        for t in range(Q_TILES):
+            for k in range(2):
+                quantised[k, t] = quantise_query(k, t)
+
+        def score_plane(k, t, evict):
+            plane = held.tile([P, T], F32, name=f"plane{k}_{t}", tag=f"plane{k}_{t}")
+            q_words, q_scales = quantised[k, t]
+            for n in range(KEY_CHUNKS):
+                acc = bank(k * KEY_CHUNKS + n)
+                nc.tensor.matmul_mx(
+                    out=acc[:],
+                    lhsT=q_words[:].bitcast(FP8X4),
+                    lhsT_scale=q_scales[:],
+                    rhs=key_words[n // 2][:, (n % 2) * BANK : (n % 2 + 1) * BANK].bitcast(FP8X4),
+                    rhs_scale=key_scales[:, n * BANK : (n + 1) * BANK],
+                    start=True,
+                    stop=True,
+                )
+                evict[n % len(evict)](plane[:, n * BANK : (n + 1) * BANK], acc[:])
+            return plane
+
+        def turn_sum(dst, parts):
+            for b in range(dst.shape[1] // P):
+                cols = slice(b * P, (b + 1) * P)
+                for n, part in enumerate(parts):
+                    nc.tensor.matmul(
+                        out=dst[:, cols], lhsT=part[:, cols], rhs=ident[:], is_transpose=True,
+                        start=(n == 0), stop=(n == len(parts) - 1),
+                    )
+
+        first = [held.tile([P, 2, I], F32, name=f"first{t}", tag=f"first{t}") for t in range(Q_TILES)]
+        second = [held.tile([P, 2, I], F32, name=f"second{t}", tag=f"second{t}") for t in range(Q_TILES)]
+
+        def look_up(points, lst, k, plane, gather):
+            gather(points[:, k, :], plane[:].indirect(lst[:]))
+
+        def products(t, h):
+            slots = slice(h * HALF, (h + 1) * HALF)
+            parts = work.tile([P, 4, HALF], F32, name="parts", bufs=4)
+            one, two = first[t], second[t]
+            nc.vector.tensor_tensor(out=parts[:, 0:2, :], in0=one[:, :, slots], in1=two[:, :, slots], op=ALU.mult)
+            nc.vector.tensor_tensor(out=parts[:, 2, :], in0=one[:, 0, slots], in1=two[:, 1, slots], op=ALU.mult)
+            nc.vector.scalar_tensor_tensor(
+                out=parts[:, 3, :], in0=one[:, 1, slots], scalar=-1.0, in1=two[:, 0, slots],
+                op0=ALU.mult, op1=ALU.mult,
+            )
+            turned = bank(7 - 2 * t - h)
+            turn_sum(turned[:, 0:HALF], [parts[:, 0, :], parts[:, 1, :]])
+            turn_sum(turned[:, HALF:I], [parts[:, 2, :], parts[:, 3, :]])
+            return turned
+
+        squares = []
+
+        def square(t, h, turned):
+            if h == 0:
+                squares.append(held.tile([P, 3, I], F32, name=f"squares{t}", tag=f"plane1_{1 - t}"))
+            nc.scalar.activation(out=squares[t][:, h, :], in_=turned[:], func=ACT.Square)
+            den = work.tile([P, HALF], F32, name="den", bufs=4)
+            nc.vector.tensor_tensor(
+                out=den[:], in0=squares[t][:, h, 0:HALF], in1=squares[t][:, h, HALF:I], op=ALU.add
+            )
+            return den
+
+        def inverse_length(t, h, den):
+            inv_len = held.tile([P, HALF], F32, name=f"inv_len{t}_{h}", tag=f"inv_len{t}_{h}")
+            nc.scalar.activation(out=inv_len[:], in_=den[:], func=ACT.Abs_reciprocal_sqrt, bias=half_col[:])
+            return inv_len
+
+        def cosine(t, turned, inv_len):
+            cos_t = held.tile([P, I], F32, name=f"cos_t{t}", tag=("first1", "first0")[t])
+            cos = bank(3 - t)
+            for h in range(2):
+                slots = slice(h * HALF, (h + 1) * HALF)
+                nc.vector.tensor_tensor(out=cos_t[:, slots], in0=turned[h][:, 0:HALF], in1=inv_len[h][:], op=ALU.mult)
+                turn_sum(cos[:, slots], [cos_t[:, slots]])
+            return cos
+
+        def exponentiate(t, cos):
+            p = work.tile([P, PACK, P], F32, name="p")
+            z0 = held.tile([P, 1], F32, name=f"z0_{t}", tag=("half_col", "z1")[t])
+            nc.scalar.activation(
+                out=p[:], in_=cos[:].rearrange("p (s j) -> p j s", j=PACK), func=ACT.Exp,
+                scale=lam_sb[t][:], accum_out=z0[:],
+            )
+            return p, z0
+
+        v_woven = held.tile([P, E, PACK], BF16, name="v_woven", align_bytes=64)
+
+        def turn_values(picked, pair, evict):
+            turned = bank(3 - pair)
+            for n in range(2):
+                words = picked[2 * pair + n].bitcast(F32)
+                for u in range(2):
+                    nc.tensor.transpose(
+                        turned[:, (2 * n + u) * P : (2 * n + u + 1) * P], words[:, u : 2 * P : 2], ident[:]
+                    )
+            dst = v_woven[:].rearrange("p e j -> p (e j)").bitcast(F32)[:, pair * BANK : (pair + 1) * BANK]
+            evict(
+                dst.rearrange("p (n e u) -> p n e u", n=2, u=2),
+                turned[:].rearrange("p (n u e) -> p n e u", n=2, u=2),
+            )
+
+        def run_sums(t, p, z0):
+            run_sum = work.tile([P, G], F32, name="run_sum")
+            nc.vector.tensor_reduce(
+                out=run_sum[:], in_=p[:].rearrange("p j (g h) -> p g j h", h=2), axis=AXIS.XY, op=ALU.add
+            )
+            outside = work.tile([P, G], F32, name="outside")
+            nc.vector.tensor_scalar(
+                out=outside[:], in0=run_sum[:], scalar1=-1.0, scalar2=z0[:], op0=ALU.mult, op1=ALU.add
+            )
+            k0 = work.tile([P, G], F32, name="k0")
+            nc.vector.reciprocal(out=k0[:], in_=outside[:])
+            k0_twice = work.tile([P, G, 2], F32, name="k0_twice")
+            nc.vector.tensor_copy(out=k0_twice[:], in_=k0[:].unsqueeze(2).to_broadcast([P, G, 2]))
+            k0_t = bank(6 - t)
+            nc.tensor.transpose(k0_t[:, 0:P], k0_twice[:].rearrange("p g h -> p (g h)"), ident[:])
+            return k0_t
+
+        def turn_scaled(t, p):
+            p_t = bank(t)
+            for j in range(PACK):
+                nc.tensor.transpose(p_t[:, j * P : (j + 1) * P], p[:, j, :], ident[:])
+            scaled = work.tile([P, PACK, P], F32, name="scaled")
+            for j in range(PACK):
+                nc.scalar.activation(
+                    out=scaled[:, j, :], in_=p_t[:, j * P : (j + 1) * P], func=ACT.Copy, scale=os_sb[:, j : j + 1]
+                )
+            return scaled
+
+        def weights(scaled, k0_t):
+            w_woven = work.tile([P, P, PACK], BF16, name="w_woven", align_bytes=64)
+            nc.vector.tensor_tensor(
+                out=w_woven[:],
+                in0=scaled[:].rearrange("p j q -> p q j"),
+                in1=k0_t[:, 0:P].unsqueeze(2).to_broadcast([P, P, PACK]),
+                op=ALU.mult,
+            )
+            w_words = work.tile([P, P], U32, name="w_words", align_bytes=64)
+            w_scales = work.tile([P, P], U8, name="w_scales", align_bytes=64)
+            nc.vector.quantize_mx(
+                out=w_words[:].bitcast(FP8X4), scales=w_scales[:], in_=w_woven[:].rearrange("p q j -> p (q j)")
+            )
+            return w_words, w_scales
+
+        def gather_members(t):
+            rows = list3[:, t * (P // 16) : (t + 1) * (P // 16)]
+            mine = held.tile([P, E_TILES + 1, P], F32, name=f"mine{t}", tag=f"lam{t}")
+            scalar_move(mine[:, E_TILES, :], mgain_sb[:].indirect(rows))
+            for c in range(E_TILES):
+                scalar_move(mine[:, c, :], member_sb[c][:].indirect(rows))
+            return mine
+
+        v_words = held.tile([P, E], U32, name="v_words", align_bytes=64)
+        v_scales = held.tile([P, E], U8, name="v_scales", align_bytes=64)
+
+        def read_out(t, w_words, w_scales, mine):
+            cols = slice(t * P, (t + 1) * P)
+            o = bank(7 - 3 * t)
+            for c in range(E_TILES):
+                e_cols = slice(c * P, (c + 1) * P)
+                nc.tensor.matmul_mx(
+                    out=o[:, e_cols],
+                    lhsT=v_words[:, e_cols].bitcast(FP8X4),
+                    lhsT_scale=v_scales[:, e_cols],
+                    rhs=w_words[:].bitcast(FP8X4),
+                    rhs_scale=w_scales[:],
+                    start=True,
+                    stop=True,
+                )
+            gained = work.tile([P, E_TILES, P], F32, name="gained")
+            nc.vector.tensor_tensor(
+                out=gained[:],
+                in0=o[:].rearrange("p (c q) -> p c q", q=P),
+                in1=mine[:, E_TILES, :].unsqueeze(1).to_broadcast([P, E_TILES, P]),
+                op=ALU.mult,
+            )
+            y = work.tile([P, E_TILES, P], F32, name="y")
+            nc.vector.tensor_tensor(out=y[:], in0=gained[:], in1=mine[:, 0:E_TILES, :], op=ALU.add)
+            nc.sync.dma_start(out=out.rearrange("(c p) q -> p c q", p=P)[:, :, cols], in_=y[:])
+
+        a0 = score_plane(0, 0, (scalar_move, vector_copy))
+        b0 = score_plane(1, 0, (scalar_copy,))
+        for k, plane in enumerate((a0, b0)):
+            look_up(first[0], list1, k, plane, vector_copy)
+            look_up(second[0], list2, k, plane, vector_copy)
+        a1 = score_plane(0, 1, (scalar_copy,))
+        b1 = score_plane(1, 1, (scalar_copy,))
+        turned0 = [products(0, h) for h in range(2)]
+        for k, (plane, gather) in enumerate(((a1, vector_copy), (b1, scalar_move))):
+            look_up(first[1], list1, k, plane, gather)
+            look_up(second[1], list2, k, plane, gather)
+
+        def pick_values(dst, c, gather):
+            gather(dst, vals_sb[c][:].indirect(list1[:]))
+            return dst
+
+        turned1 = [products(1, 0)]
+        den0 = [square(0, h, turned0[h]) for h in range(2)]
+        turned1.append(products(1, 1))
+        picked = [pick_values(squares[0][:, 2, 0:HALF].bitcast(BF16), 0, scalar_move)]
+        inv_len0 = [inverse_length(0, h, den0[h]) for h in range(2)]
+        den1 = [square(1, h, turned1[h]) for h in range(2)]
+        inv_len1 = [inverse_length(1, h, den1[h]) for h in range(2)]
+        pick1 = held.tile([P, I], BF16, name="pick1", tag="second1")
+        picked.append(pick_values(pick1[:], 1, vector_copy))
+        cos0 = cosine(0, turned0, inv_len0)
+        cos1 = cosine(1, turned1, inv_len1)
+        soft = [exponentiate(0, cos0), exponentiate(1, cos1)]
+        pick23 = held.tile([P, 2, I], BF16, name="pick23", tag="inv_len1_1")
+        picked.extend(pick_values(pick23[:, n, :], 2 + n, vector_copy) for n in range(2))
+        k0_t0 = run_sums(0, *soft[0])
+        scaled0 = turn_scaled(0, soft[0][0])
+        k0_t1 = run_sums(1, *soft[1])
+        for pair in range(2):
+            turn_values(picked, pair, scalar_copy)
+        w0 = weights(scaled0, k0_t0)
+        nc.vector.quantize_mx(
+            out=v_words[:].bitcast(FP8X4), scales=v_scales[:], in_=v_woven[:].rearrange("p e j -> p (e j)")
+        )
+        scaled1 = turn_scaled(1, soft[1][0])
+        w1 = weights(scaled1, k0_t1)
+        read_out(0, *w0, gather_members(0))
+        read_out(1, *w1, gather_members(1))

@@ -59,16 +59,16 @@ def tile_attend_planecos_outside_bymember_kernel(
         raw_q = [
             [held.tile([P, PACK, P], F32, name=f"raw_q{k}_{t}") for t in range(Q_TILES)] for k in range(2)
         ]
-        key_words = [held.tile([P, T // 2], U32, name=f"key_words{n}", align_bytes=64) for n in range(2)]
+        key_words = [held.tile([P, BANK], U32, name=f"key_words{n}", align_bytes=64) for n in range(KEY_CHUNKS)]
 
         def load_query(k, t):
             rows = (query, query2)[k].rearrange("(p j) w -> p j w", j=PACK)
             nc.sync.dma_start(out=raw_q[k][t][:], in_=rows[:, :, t * P : (t + 1) * P])
 
-        load_query(0, 0)
-        for n in range(2):
-            nc.sync.dma_start(out=key_words[n][:].bitcast(I32), in_=words_hbm[:, n * T // 2 : (n + 1) * T // 2])
-        load_query(1, 0)
+        for n in range(KEY_CHUNKS):
+            if n % 2 == 0:
+                load_query(n // 2, 0)
+            nc.sync.dma_start(out=key_words[n][:].bitcast(I32), in_=words_hbm[:, n * BANK : (n + 1) * BANK])
         list1 = held.tile([P, I // 16], U16, name="list1")
         list2 = held.tile([P, I // 16], U16, name="list2")
         list3 = held.tile([P, Q // 16], U16, name="list3")
@@ -80,6 +80,11 @@ def tile_attend_planecos_outside_bymember_kernel(
         for c in range(E_TILES):
             nc.sync.dma_start(out=vals_sb[c][:], in_=vals[c * P : (c + 1) * P, :])
         nc.sync.dma_start(list3[:], offs3)
+        lam_sb = [held.tile([P, 1], F32, name=f"lam{t}", tag=f"lam{t}", align_bytes=64) for t in range(Q_TILES)]
+        for t in range(Q_TILES):
+            nc.sync.dma_start(out=lam_sb[t][:], in_=lam[t * P : (t + 1) * P, :])
+        os_sb = held.tile([P, PACK], F32, name="os_sb")
+        nc.sync.dma_start(out=os_sb[:], in_=slot_factor.rearrange("o (p j) -> (o p) j", j=PACK))
         mgain_sb = held.tile([P, M], F32, name="mgain_sb")
         nc.sync.dma_start(out=mgain_sb[:], in_=mgain)
         member_sb = [held.tile([P, M], F32, name=f"member{c}") for c in range(E_TILES)]
@@ -90,14 +95,10 @@ def tile_attend_planecos_outside_bymember_kernel(
         make_identity(nc, ident[:])
         half_col = held.tile([P, 1], F32, name="half_col", tag="half_col")
         nc.gpsimd.memset(half_col[:], 0.5)
-        lam_sb = [held.tile([P, 1], F32, name=f"lam{t}", tag=f"lam{t}") for t in range(Q_TILES)]
-        for t in range(Q_TILES):
-            nc.gpsimd.dma_start(out=lam_sb[t][:], in_=lam[t * P : (t + 1) * P, :])
-        os_sb = held.tile([P, PACK], F32, name="os_sb")
-        nc.gpsimd.dma_start(out=os_sb[:], in_=slot_factor.rearrange("o (p j) -> (o p) j", j=PACK))
 
         def quantise_query(k, t):
-            woven = held.tile([P, P, PACK], BF16, name=f"q_woven{k}_{t}", align_bytes=64)
+            tag = f"points{k}_0" if t == 1 else f"q_woven{k}"
+            woven = held.tile([P, P, PACK], BF16, name=f"q_woven{k}_{t}", tag=tag, align_bytes=64)
             vector_copy(
                 woven[:].rearrange("p (c i) j -> p c j i", i=4),
                 raw_q[k][t][:].rearrange("p j (c i) -> p c j i", i=4),
@@ -123,7 +124,7 @@ def tile_attend_planecos_outside_bymember_kernel(
                     out=acc[:],
                     lhsT=q_words[:].bitcast(FP8X4),
                     lhsT_scale=q_scales[:],
-                    rhs=key_words[n // 2][:, (n % 2) * BANK : (n % 2 + 1) * BANK].bitcast(FP8X4),
+                    rhs=key_words[n][:].bitcast(FP8X4),
                     rhs_scale=key_scales[:, n * BANK : (n + 1) * BANK],
                     start=True,
                     stop=True,
@@ -140,20 +141,25 @@ def tile_attend_planecos_outside_bymember_kernel(
                         start=(n == 0), stop=(n == len(parts) - 1),
                     )
 
-        first = [held.tile([P, 2, I], F32, name=f"first{t}", tag=f"first{t}") for t in range(Q_TILES)]
-        second = [held.tile([P, 2, I], F32, name=f"second{t}", tag=f"second{t}") for t in range(Q_TILES)]
+        points = {
+            (k, t): held.tile([P, 2, I], F32, name=f"points{k}_{t}", tag=f"points{k}_{t}", align_bytes=64)
+            for t in range(Q_TILES)
+            for k in range(2)
+        }
+        lists = (list1, list2)
 
-        def look_up(points, lst, k, plane, gather):
-            gather(points[:, k, :], plane[:].indirect(lst[:]))
+        def look_up(k, t, n, plane, gather):
+            gather(points[k, t][:, n, :], plane[:].indirect(lists[n][:]))
 
         def products(t, h):
             slots = slice(h * HALF, (h + 1) * HALF)
             parts = work.tile([P, 4, HALF], F32, name="parts", bufs=4)
-            one, two = first[t], second[t]
-            nc.vector.tensor_tensor(out=parts[:, 0:2, :], in0=one[:, :, slots], in1=two[:, :, slots], op=ALU.mult)
-            nc.vector.tensor_tensor(out=parts[:, 2, :], in0=one[:, 0, slots], in1=two[:, 1, slots], op=ALU.mult)
+            a, b = points[0, t], points[1, t]
+            nc.vector.tensor_tensor(out=parts[:, 0, :], in0=a[:, 0, slots], in1=a[:, 1, slots], op=ALU.mult)
+            nc.vector.tensor_tensor(out=parts[:, 1, :], in0=b[:, 0, slots], in1=b[:, 1, slots], op=ALU.mult)
+            nc.vector.tensor_tensor(out=parts[:, 2, :], in0=a[:, 0, slots], in1=b[:, 1, slots], op=ALU.mult)
             nc.vector.scalar_tensor_tensor(
-                out=parts[:, 3, :], in0=one[:, 1, slots], scalar=-1.0, in1=two[:, 0, slots],
+                out=parts[:, 3, :], in0=b[:, 0, slots], scalar=-1.0, in1=a[:, 1, slots],
                 op0=ALU.mult, op1=ALU.mult,
             )
             turned = bank(7 - 2 * t - h)
@@ -179,7 +185,7 @@ def tile_attend_planecos_outside_bymember_kernel(
             return inv_len
 
         def cosine(t, turned, inv_len):
-            cos_t = held.tile([P, I], F32, name=f"cos_t{t}", tag=("first1", "first0")[t])
+            cos_t = held.tile([P, I], F32, name=f"cos_t{t}", tag=("plane1_0", "cos_t1")[t])
             cos = bank(3 - t)
             for h in range(2):
                 slots = slice(h * HALF, (h + 1) * HALF)
@@ -196,7 +202,8 @@ def tile_attend_planecos_outside_bymember_kernel(
             )
             return p, z0
 
-        v_woven = held.tile([P, E, PACK], BF16, name="v_woven", align_bytes=64)
+        v_words = held.tile([P, E], U32, name="v_words", align_bytes=64)
+        v_scales = held.tile([P, E], U8, name="v_scales", align_bytes=64)
 
         def turn_values(picked, pair, evict):
             turned = bank(3 - pair)
@@ -206,45 +213,53 @@ def tile_attend_planecos_outside_bymember_kernel(
                     nc.tensor.transpose(
                         turned[:, (2 * n + u) * P : (2 * n + u + 1) * P], words[:, u : 2 * P : 2], ident[:]
                     )
-            dst = v_woven[:].rearrange("p e j -> p (e j)").bitcast(F32)[:, pair * BANK : (pair + 1) * BANK]
+            woven = held.tile(
+                [P, 2 * P * PACK], BF16, name=f"v_woven{pair}", tag=("v_woven0", "lam1")[pair], align_bytes=64
+            )
             evict(
-                dst.rearrange("p (n e u) -> p n e u", n=2, u=2),
+                woven[:].bitcast(F32).rearrange("p (n e u) -> p n e u", n=2, u=2),
                 turned[:].rearrange("p (n u e) -> p n e u", n=2, u=2),
             )
+            cols = slice(pair * 2 * P, (pair + 1) * 2 * P)
+            nc.vector.quantize_mx(out=v_words[:, cols].bitcast(FP8X4), scales=v_scales[:, cols], in_=woven[:])
 
-        def run_sums(t, p, z0):
+        def run_sums(p):
             run_sum = work.tile([P, G], F32, name="run_sum")
             nc.vector.tensor_reduce(
                 out=run_sum[:], in_=p[:].rearrange("p j (g h) -> p g j h", h=2), axis=AXIS.XY, op=ALU.add
             )
-            outside = work.tile([P, G], F32, name="outside")
-            nc.vector.tensor_scalar(
-                out=outside[:], in0=run_sum[:], scalar1=-1.0, scalar2=z0[:], op0=ALU.mult, op1=ALU.add
-            )
-            k0 = work.tile([P, G], F32, name="k0")
-            nc.vector.reciprocal(out=k0[:], in_=outside[:])
-            k0_twice = work.tile([P, G, 2], F32, name="k0_twice")
-            nc.vector.tensor_copy(out=k0_twice[:], in_=k0[:].unsqueeze(2).to_broadcast([P, G, 2]))
-            k0_t = bank(6 - t)
-            nc.tensor.transpose(k0_t[:, 0:P], k0_twice[:].rearrange("p g h -> p (g h)"), ident[:])
-            return k0_t
+            return run_sum
 
         def turn_scaled(t, p):
             p_t = bank(t)
-            for j in range(PACK):
-                nc.tensor.transpose(p_t[:, j * P : (j + 1) * P], p[:, j, :], ident[:])
-            scaled = work.tile([P, PACK, P], F32, name="scaled")
-            for j in range(PACK):
-                nc.scalar.activation(
-                    out=scaled[:, j, :], in_=p_t[:, j * P : (j + 1) * P], func=ACT.Copy, scale=os_sb[:, j : j + 1]
-                )
+            turn_sum(p_t[:], [p[:].rearrange("p j s -> p (j s)")])
+            scaled = work.tile([P, P, PACK], F32, name="scaled")
+            nc.vector.tensor_tensor(
+                out=scaled[:],
+                in0=p_t[:].rearrange("p (j q) -> p q j", j=PACK),
+                in1=os_sb[:].unsqueeze(1).to_broadcast([P, P, PACK]),
+                op=ALU.mult,
+            )
             return scaled
+
+        def inverse_outside(t, run_sum, z0):
+            root = held.tile([P, G], F32, name=f"root{t}", tag=("lam1", "root1")[t], align_bytes=64)
+            nc.scalar.activation(
+                out=root[:], in_=run_sum[:], func=ACT.Abs_reciprocal_sqrt, scale=-1.0, bias=z0[:]
+            )
+            k0_twice = work.tile([P, G, 2], F32, name="k0_twice")
+            nc.scalar.activation(
+                out=k0_twice[:], in_=root[:].unsqueeze(2).to_broadcast([P, G, 2]), func=ACT.Square
+            )
+            k0_t = bank(6 - t)
+            nc.tensor.transpose(k0_t[:, 0:P], k0_twice[:].rearrange("p g h -> p (g h)"), ident[:])
+            return k0_t
 
         def weights(scaled, k0_t):
             w_woven = work.tile([P, P, PACK], BF16, name="w_woven", align_bytes=64)
             nc.vector.tensor_tensor(
                 out=w_woven[:],
-                in0=scaled[:].rearrange("p j q -> p q j"),
+                in0=scaled[:],
                 in1=k0_t[:, 0:P].unsqueeze(2).to_broadcast([P, P, PACK]),
                 op=ALU.mult,
             )
@@ -255,16 +270,12 @@ def tile_attend_planecos_outside_bymember_kernel(
             )
             return w_words, w_scales
 
-        def gather_members(t):
-            rows = list3[:, t * (P // 16) : (t + 1) * (P // 16)]
-            mine = held.tile([P, E_TILES + 1, P], F32, name=f"mine{t}", tag=f"lam{t}")
-            scalar_move(mine[:, E_TILES, :], mgain_sb[:].indirect(rows))
+        def gather_members():
+            mine = held.tile([P, E_TILES + 1, Q], F32, name="mine", tag="root1", align_bytes=64)
+            scalar_move(mine[:, E_TILES, :], mgain_sb[:].indirect(list3[:]))
             for c in range(E_TILES):
-                scalar_move(mine[:, c, :], member_sb[c][:].indirect(rows))
+                scalar_move(mine[:, c, :], member_sb[c][:].indirect(list3[:]))
             return mine
-
-        v_words = held.tile([P, E], U32, name="v_words", align_bytes=64)
-        v_scales = held.tile([P, E], U8, name="v_scales", align_bytes=64)
 
         def read_out(t, w_words, w_scales, mine):
             cols = slice(t * P, (t + 1) * P)
@@ -284,24 +295,25 @@ def tile_attend_planecos_outside_bymember_kernel(
             nc.vector.tensor_tensor(
                 out=gained[:],
                 in0=o[:].rearrange("p (c q) -> p c q", q=P),
-                in1=mine[:, E_TILES, :].unsqueeze(1).to_broadcast([P, E_TILES, P]),
+                in1=mine[:, E_TILES, cols].unsqueeze(1).to_broadcast([P, E_TILES, P]),
                 op=ALU.mult,
             )
             y = work.tile([P, E_TILES, P], F32, name="y")
-            nc.vector.tensor_tensor(out=y[:], in0=gained[:], in1=mine[:, 0:E_TILES, :], op=ALU.add)
+            nc.vector.tensor_tensor(out=y[:], in0=gained[:], in1=mine[:, 0:E_TILES, cols], op=ALU.add)
             nc.sync.dma_start(out=out.rearrange("(c p) q -> p c q", p=P)[:, :, cols], in_=y[:])
 
         a0 = score_plane(0, 0, (scalar_move, vector_copy))
         b0 = score_plane(1, 0, (scalar_copy,))
         for k, plane in enumerate((a0, b0)):
-            look_up(first[0], list1, k, plane, vector_copy)
-            look_up(second[0], list2, k, plane, vector_copy)
+            for n in range(2):
+                look_up(k, 0, n, plane, vector_copy)
         a1 = score_plane(0, 1, (scalar_copy,))
         b1 = score_plane(1, 1, (scalar_copy,))
         turned0 = [products(0, h) for h in range(2)]
-        for k, (plane, gather) in enumerate(((a1, vector_copy), (b1, scalar_move))):
-            look_up(first[1], list1, k, plane, gather)
-            look_up(second[1], list2, k, plane, gather)
+        look_up(0, 1, 0, a1, vector_copy)
+        look_up(0, 1, 1, a1, scalar_move)
+        for n in range(2):
+            look_up(1, 1, n, b1, scalar_move)
 
         def pick_values(dst, c, gather):
             gather(dst, vals_sb[c][:].indirect(list1[:]))
@@ -314,23 +326,22 @@ def tile_attend_planecos_outside_bymember_kernel(
         inv_len0 = [inverse_length(0, h, den0[h]) for h in range(2)]
         den1 = [square(1, h, turned1[h]) for h in range(2)]
         inv_len1 = [inverse_length(1, h, den1[h]) for h in range(2)]
-        pick1 = held.tile([P, I], BF16, name="pick1", tag="second1")
+        pick1 = held.tile([P, I], BF16, name="pick1", tag="points1_1", align_bytes=64)
         picked.append(pick_values(pick1[:], 1, vector_copy))
         cos0 = cosine(0, turned0, inv_len0)
         cos1 = cosine(1, turned1, inv_len1)
         soft = [exponentiate(0, cos0), exponentiate(1, cos1)]
-        pick23 = held.tile([P, 2, I], BF16, name="pick23", tag="inv_len1_1")
-        picked.extend(pick_values(pick23[:, n, :], 2 + n, vector_copy) for n in range(2))
-        k0_t0 = run_sums(0, *soft[0])
-        scaled0 = turn_scaled(0, soft[0][0])
-        k0_t1 = run_sums(1, *soft[1])
-        for pair in range(2):
-            turn_values(picked, pair, scalar_copy)
-        w0 = weights(scaled0, k0_t0)
-        nc.vector.quantize_mx(
-            out=v_words[:].bitcast(FP8X4), scales=v_scales[:], in_=v_woven[:].rearrange("p e j -> p (e j)")
-        )
-        scaled1 = turn_scaled(1, soft[1][0])
-        w1 = weights(scaled1, k0_t1)
-        read_out(0, *w0, gather_members(0))
-        read_out(1, *w1, gather_members(1))
+        pick2 = held.tile([P, I], BF16, name="pick2", tag="inv_len1_0")
+        picked.append(pick_values(pick2[:], 2, vector_copy))
+        pick3 = held.tile([P, I], BF16, name="pick3", tag="inv_len1_1")
+        picked.append(pick_values(pick3[:], 3, vector_copy))
+        sums = [run_sums(p) for p, z0 in soft]
+        k0_t = [inverse_outside(t, sums[t], soft[t][1]) for t in range(Q_TILES)]
+        scaled = [turn_scaled(t, soft[t][0]) for t in range(Q_TILES)]
+        turn_values(picked, 0, vector_copy)
+        turn_values(picked, 1, scalar_copy)
+        w0 = weights(scaled[0], k0_t[0])
+        w1 = weights(scaled[1], k0_t[1])
+        mine = gather_members()
+        read_out(0, *w0, mine)
+        read_out(1, *w1, mine)

@@ -96,6 +96,9 @@ def tile_attend_planecos_outside_bymember_kernel(
         half_col = held.tile([P, 1], F32, name="half_col", tag="half_col")
         nc.gpsimd.memset(half_col[:], 0.5)
 
+        warm = held.tile([P, 1], F32, name="warm")
+        nc.scalar.activation(out=warm[:], in_=half_col[:], func=ACT.Abs_reciprocal_sqrt)
+
         def quantise_query(k, t):
             tag = f"points{k}_0" if t == 1 else f"q_woven{k}"
             woven = held.tile([P, P, PACK], BF16, name=f"q_woven{k}_{t}", tag=tag, align_bytes=64)

@@ -20,7 +20,10 @@ AXIS = mybir.AxisListType
 P = 128
 PACK = 4
 BANK = 512
-BANKS = 8
+QUADRANT = 32
+SCALE_ROWS = 4
+LIST_ROWS = 16
+MX_ALIGN = 64
 Q_TILES = Q // P
 E_TILES = E // P
 KEY_CHUNKS = T // BANK
@@ -45,42 +48,42 @@ def tile_attend_planecos_outside_bymember_kernel(
         def scalar_copy(dst, src):
             nc.scalar.copy(out=dst, in_=src)
 
-        def scalar_move(dst, src):
+        def scalar_gather(dst, src):
             nc.scalar.activation(out=dst, in_=src, func=ACT.Copy)
 
-        key_scales = held.tile([P, T], U8, name="key_scales", align_bytes=64)
+        key_scales = held.tile([P, BANK], U8, name="key_scales", align_bytes=MX_ALIGN)
         nc.gpsimd.memset(key_scales[:].bitcast(U32), 0)
-        for quad in range(4):
+        for quad in range(P // QUADRANT):
+            scale_rows = keys_scales[0, SCALE_ROWS * quad : SCALE_ROWS * (quad + 1), :]
             nc.sync.dma_start(
-                out=key_scales[32 * quad : 32 * quad + 4, :].bitcast(I32),
-                in_=keys_scales[0, 4 * quad : 4 * quad + 4, :].bitcast(I32),
+                out=key_scales[QUADRANT * quad : QUADRANT * quad + SCALE_ROWS * KEY_CHUNKS, :].bitcast(I32),
+                in_=scale_rows.rearrange("r (n c) -> n r c", n=KEY_CHUNKS).bitcast(I32),
             )
         words_hbm = keys_words[0].rearrange("p n t -> p (n t)").bitcast(I32)
-        raw_q = [
-            [held.tile([P, PACK, P], F32, name=f"raw_q{k}_{t}") for t in range(Q_TILES)] for k in range(2)
+        raw_q = [held.tile([P, PACK, Q], F32, name=f"raw_q{k}") for k in range(2)]
+        key_words = [
+            held.tile([P, BANK], U32, name=f"key_words{n}", align_bytes=MX_ALIGN) for n in range(KEY_CHUNKS)
         ]
-        key_words = [held.tile([P, BANK], U32, name=f"key_words{n}", align_bytes=64) for n in range(KEY_CHUNKS)]
 
-        def load_query(k, t):
-            rows = (query, query2)[k].rearrange("(p j) w -> p j w", j=PACK)
-            nc.sync.dma_start(out=raw_q[k][t][:], in_=rows[:, :, t * P : (t + 1) * P])
+        def load_query(k):
+            nc.sync.dma_start(out=raw_q[k][:], in_=(query, query2)[k].rearrange("(p j) w -> p j w", j=PACK))
 
+        load_query(0)
         for n in range(KEY_CHUNKS):
-            if n % 2 == 0:
-                load_query(n // 2, 0)
             nc.sync.dma_start(out=key_words[n][:].bitcast(I32), in_=words_hbm[:, n * BANK : (n + 1) * BANK])
-        list1 = held.tile([P, I // 16], U16, name="list1")
-        list2 = held.tile([P, I // 16], U16, name="list2")
-        list3 = held.tile([P, Q // 16], U16, name="list3")
+        load_query(1)
+        list1 = held.tile([P, I // LIST_ROWS], U16, name="list1")
+        list2 = held.tile([P, I // LIST_ROWS], U16, name="list2")
+        list3 = held.tile([P, Q // LIST_ROWS], U16, name="list3")
         nc.sync.dma_start(list1[:], offs)
         nc.sync.dma_start(list2[:], offs2)
-        load_query(0, 1)
-        load_query(1, 1)
         vals_sb = [held.tile([P, T], F32, name=f"vals{c}") for c in range(E_TILES)]
         for c in range(E_TILES):
             nc.sync.dma_start(out=vals_sb[c][:], in_=vals[c * P : (c + 1) * P, :])
         nc.sync.dma_start(list3[:], offs3)
-        lam_sb = [held.tile([P, 1], F32, name=f"lam{t}", tag=f"lam{t}", align_bytes=64) for t in range(Q_TILES)]
+        lam_sb = [
+            held.tile([P, 1], F32, name=f"lam{t}", tag=f"lam{t}", align_bytes=MX_ALIGN) for t in range(Q_TILES)
+        ]
         for t in range(Q_TILES):
             nc.sync.dma_start(out=lam_sb[t][:], in_=lam[t * P : (t + 1) * P, :])
         os_sb = held.tile([P, PACK], F32, name="os_sb")
@@ -93,138 +96,147 @@ def tile_attend_planecos_outside_bymember_kernel(
 
         ident = held.tile([P, P], F32, name="ident")
         make_identity(nc, ident[:])
-        half_col = held.tile([P, 1], F32, name="half_col", tag="half_col")
-        nc.gpsimd.memset(half_col[:], 0.5)
+        one_half = held.tile([P, 1], F32, name="one_half", tag="one_half")
+        nc.gpsimd.memset(one_half[:], 0.5)
 
         warm = held.tile([P, 1], F32, name="warm")
-        nc.scalar.activation(out=warm[:], in_=half_col[:], func=ACT.Abs_reciprocal_sqrt)
+        nc.scalar.activation(out=warm[:], in_=one_half[:], func=ACT.Abs_reciprocal_sqrt)
 
         def quantise_query(k, t):
-            tag = f"points{k}_0" if t == 1 else f"q_woven{k}"
-            woven = held.tile([P, P, PACK], BF16, name=f"q_woven{k}_{t}", tag=tag, align_bytes=64)
+            tag = "points0_0_0" if (k, t) == (1, Q_TILES - 1) else f"q_woven{k}_{t}"
+            woven = held.tile([P, P, PACK], BF16, name=f"q_woven{k}_{t}", tag=tag, align_bytes=MX_ALIGN)
             vector_copy(
                 woven[:].rearrange("p (c i) j -> p c j i", i=4),
-                raw_q[k][t][:].rearrange("p j (c i) -> p c j i", i=4),
+                raw_q[k][:, :, t * P : (t + 1) * P].rearrange("p j (c i) -> p c j i", i=4),
             )
-            words = held.tile([P, P], U32, name=f"q_words{k}_{t}", align_bytes=64)
-            scales = held.tile([P, P], U8, name=f"q_scales{k}_{t}", align_bytes=64)
+            words = held.tile([P, P], U32, name=f"q_words{k}_{t}", align_bytes=MX_ALIGN)
+            scales = held.tile([P, P], U8, name=f"q_scales{k}_{t}", align_bytes=MX_ALIGN)
             nc.vector.quantize_mx(
                 out=words[:].bitcast(FP8X4), scales=scales[:], in_=woven[:].rearrange("p w j -> p (w j)")
             )
             return words, scales
 
-        quantised = {}
-        for t in range(Q_TILES):
-            for k in range(2):
-                quantised[k, t] = quantise_query(k, t)
+        quantised = {(k, t): quantise_query(k, t) for k in range(2) for t in range(Q_TILES)}
 
-        def score_plane(k, t, evict):
+        def score_plane(k, t):
             plane = held.tile([P, T], F32, name=f"plane{k}_{t}", tag=f"plane{k}_{t}")
             q_words, q_scales = quantised[k, t]
             for n in range(KEY_CHUNKS):
-                acc = bank(k * KEY_CHUNKS + n)
+                acc = bank(t * KEY_CHUNKS + n)
                 nc.tensor.matmul_mx(
                     out=acc[:],
                     lhsT=q_words[:].bitcast(FP8X4),
                     lhsT_scale=q_scales[:],
                     rhs=key_words[n][:].bitcast(FP8X4),
-                    rhs_scale=key_scales[:, n * BANK : (n + 1) * BANK],
+                    rhs_scale=key_scales[SCALE_ROWS * n : P, :],
                     start=True,
                     stop=True,
                 )
-                evict[n % len(evict)](plane[:, n * BANK : (n + 1) * BANK], acc[:])
+                empty = vector_copy if (k, t, n) == (0, 0, 1) else scalar_copy
+                empty(plane[:, n * BANK : (n + 1) * BANK], acc[:])
             return plane
 
-        def turn_sum(dst, parts):
-            for b in range(dst.shape[1] // P):
-                cols = slice(b * P, (b + 1) * P)
-                for n, part in enumerate(parts):
-                    nc.tensor.matmul(
-                        out=dst[:, cols], lhsT=part[:, cols], rhs=ident[:], is_transpose=True,
-                        start=(n == 0), stop=(n == len(parts) - 1),
-                    )
+        planes = {(k, t): score_plane(k, t) for k in range(2) for t in range(Q_TILES)}
 
-        points = {
-            (k, t): held.tile([P, 2, I], F32, name=f"points{k}_{t}", tag=f"points{k}_{t}", align_bytes=64)
-            for t in range(Q_TILES)
-            for k in range(2)
-        }
-        lists = (list1, list2)
+        points = {}
 
-        def look_up(k, t, n, plane, gather):
-            gather(points[k, t][:, n, :], plane[:].indirect(lists[n][:]))
+        def look_up(k, t, n, gather):
+            name = f"points{k}_{t}_{n}"
+            points[k, t, n] = held.tile([P, I], F32, name=name, tag=name, align_bytes=MX_ALIGN)
+            gather(points[k, t, n][:], planes[k, t][:].indirect((list1, list2)[n][:]))
 
-        def products(t, h):
+        for k, t, n in ((0, 0, 0), (0, 0, 1), (0, 1, 0), (1, 0, 0), (1, 0, 1)):
+            look_up(k, t, n, vector_copy)
+        for k, t, n in ((0, 1, 1), (1, 1, 0), (1, 1, 1)):
+            look_up(k, t, n, scalar_gather)
+
+        def products(t, h, parts):
             slots = slice(h * HALF, (h + 1) * HALF)
-            parts = work.tile([P, 4, HALF], F32, name="parts", bufs=4)
-            a, b = points[0, t], points[1, t]
-            nc.vector.tensor_tensor(out=parts[:, 0, :], in0=a[:, 0, slots], in1=a[:, 1, slots], op=ALU.mult)
-            nc.vector.tensor_tensor(out=parts[:, 1, :], in0=b[:, 0, slots], in1=b[:, 1, slots], op=ALU.mult)
-            nc.vector.tensor_tensor(out=parts[:, 2, :], in0=a[:, 0, slots], in1=b[:, 1, slots], op=ALU.mult)
+            a1, a2, b1, b2 = (points[k, t, n][:, slots] for k in range(2) for n in range(2))
+            nc.vector.tensor_tensor(out=parts[:, 0, :], in0=a1, in1=a2, op=ALU.mult)
+            nc.vector.tensor_tensor(out=parts[:, 1, :], in0=b1, in1=b2, op=ALU.mult)
+            nc.vector.tensor_tensor(out=parts[:, 2, :], in0=a1, in1=b2, op=ALU.mult)
             nc.vector.scalar_tensor_tensor(
-                out=parts[:, 3, :], in0=b[:, 0, slots], scalar=-1.0, in1=a[:, 1, slots],
-                op0=ALU.mult, op1=ALU.mult,
+                out=parts[:, 3, :], in0=b1, scalar=-1.0, in1=a2, op0=ALU.mult, op1=ALU.mult
             )
-            turned = bank(7 - 2 * t - h)
-            turn_sum(turned[:, 0:HALF], [parts[:, 0, :], parts[:, 1, :]])
-            turn_sum(turned[:, HALF:I], [parts[:, 2, :], parts[:, 3, :]])
-            return turned
+            dot_cross_t = bank(7 - 2 * t - h)
+            passes = [(n, b) for n in (0, 3, 1, 2) for b in range(HALF // P)]
+            for n, b in passes:
+                at = (n // 2) * HALF + b * P
+                nc.tensor.matmul(
+                    out=dot_cross_t[:, at : at + P],
+                    lhsT=parts[:, n, b * P : (b + 1) * P],
+                    rhs=ident[:],
+                    is_transpose=True,
+                    start=((n, b) == passes[0]),
+                    stop=((n, b) == passes[-1]),
+                )
+            return dot_cross_t
 
-        squares = []
+        def squared_lengths(dot_cross_t, squares, lalb_t):
+            nc.scalar.activation(out=squares, in_=dot_cross_t[:], func=ACT.Square)
+            nc.vector.tensor_tensor(out=lalb_t, in0=squares[:, 0:HALF], in1=squares[:, HALF:I], op=ALU.add)
 
-        def square(t, h, turned):
-            if h == 0:
-                squares.append(held.tile([P, 3, I], F32, name=f"squares{t}", tag=f"plane1_{1 - t}"))
-            nc.scalar.activation(out=squares[t][:, h, :], in_=turned[:], func=ACT.Square)
-            den = work.tile([P, HALF], F32, name="den", bufs=4)
-            nc.vector.tensor_tensor(
-                out=den[:], in0=squares[t][:, h, 0:HALF], in1=squares[t][:, h, HALF:I], op=ALU.add
-            )
-            return den
+        def inverse_root(t, h, lalb_t):
+            inv_t = held.tile([P, HALF], F32, name=f"inv_t{t}_{h}", tag=f"inv_t{t}_{h}")
+            nc.scalar.activation(out=inv_t[:], in_=lalb_t, func=ACT.Abs_reciprocal_sqrt, bias=one_half[:])
+            return inv_t
 
-        def inverse_length(t, h, den):
-            inv_len = held.tile([P, HALF], F32, name=f"inv_len{t}_{h}", tag=f"inv_len{t}_{h}")
-            nc.scalar.activation(out=inv_len[:], in_=den[:], func=ACT.Abs_reciprocal_sqrt, bias=half_col[:])
-            return inv_len
+        def pick_values(dst, c, gather):
+            gather(dst, vals_sb[c][:].indirect(list1[:]))
+            return dst
 
-        def cosine(t, turned, inv_len):
-            cos_t = held.tile([P, I], F32, name=f"cos_t{t}", tag=("plane1_0", "cos_t1")[t])
+        def halves(tile):
+            return [tile[:, h * HALF : (h + 1) * HALF] for h in range(2)]
+
+        parts0 = held.tile([P, 2, 4, HALF], F32, name="parts0", tag="plane1_0")
+        dot_cross0 = [products(0, h, parts0[:, h]) for h in range(2)]
+        after_b1 = held.tile([P, 3, I], F32, name="after_b1", tag="plane1_1")
+        squares1 = held.tile([P, 2, I], F32, name="squares1", tag="plane1_0")
+        parts1 = held.tile([P, 2, 4, HALF], F32, name="parts1")
+        dot_cross1 = [products(1, 0, parts1[:, 0])]
+        lalb0 = halves(held.tile([P, I], F32, name="lalb0"))
+        for h in range(2):
+            squared_lengths(dot_cross0[h], after_b1[:, h, :], lalb0[h])
+        dot_cross1.append(products(1, 1, parts1[:, 1]))
+        picked = [pick_values(after_b1[:, 2, 0:HALF].bitcast(BF16), 0, scalar_gather)]
+        inv0 = [inverse_root(0, h, lalb0[h]) for h in range(2)]
+        lalb1 = halves(held.tile([P, I], F32, name="lalb1"))
+        for h in range(2):
+            squared_lengths(dot_cross1[h], squares1[:, h, :], lalb1[h])
+        inv1 = [inverse_root(1, h, lalb1[h]) for h in range(2)]
+        picked1 = held.tile([P, I], BF16, name="picked1", tag="points1_1_1", align_bytes=MX_ALIGN)
+        picked.append(pick_values(picked1[:], 1, vector_copy))
+
+        def turn(dst, src):
+            for b in range(dst.shape[1] // P):
+                nc.tensor.transpose(dst[:, b * P : (b + 1) * P], src[:, b * P : (b + 1) * P], ident[:])
+
+        def cosine(t, dot_cross_t, inv_t):
+            cos_t = held.tile([P, I], F32, name=f"cos_t{t}", tag=f"points0_{1 - t}_0", align_bytes=MX_ALIGN)
             cos = bank(3 - t)
-            for h in range(2):
-                slots = slice(h * HALF, (h + 1) * HALF)
-                nc.vector.tensor_tensor(out=cos_t[:, slots], in0=turned[h][:, 0:HALF], in1=inv_len[h][:], op=ALU.mult)
-                turn_sum(cos[:, slots], [cos_t[:, slots]])
+            for h, (src, dst) in enumerate(zip(halves(cos_t), halves(cos))):
+                nc.vector.tensor_tensor(out=src, in0=dot_cross_t[h][:, 0:HALF], in1=inv_t[h][:], op=ALU.mult)
+                turn(dst, src)
             return cos
 
         def exponentiate(t, cos):
             p = work.tile([P, PACK, P], F32, name="p")
-            z0 = held.tile([P, 1], F32, name=f"z0_{t}", tag=("half_col", "z1")[t])
+            z0 = held.tile([P, 1], F32, name=f"z0_{t}", tag=("one_half", "z0_1")[t])
             nc.scalar.activation(
-                out=p[:], in_=cos[:].rearrange("p (s j) -> p j s", j=PACK), func=ACT.Exp,
-                scale=lam_sb[t][:], accum_out=z0[:],
+                out=p[:],
+                in_=cos[:].rearrange("p (s j) -> p j s", j=PACK),
+                func=ACT.Exp,
+                scale=lam_sb[t][:],
+                accum_out=z0[:],
             )
             return p, z0
 
-        v_words = held.tile([P, E], U32, name="v_words", align_bytes=64)
-        v_scales = held.tile([P, E], U8, name="v_scales", align_bytes=64)
-
-        def turn_values(picked, pair, evict):
-            turned = bank(3 - pair)
-            for n in range(2):
-                words = picked[2 * pair + n].bitcast(F32)
-                for u in range(2):
-                    nc.tensor.transpose(
-                        turned[:, (2 * n + u) * P : (2 * n + u + 1) * P], words[:, u : 2 * P : 2], ident[:]
-                    )
-            woven = held.tile(
-                [P, 2 * P * PACK], BF16, name=f"v_woven{pair}", tag=("v_woven0", "lam1")[pair], align_bytes=64
-            )
-            evict(
-                woven[:].bitcast(F32).rearrange("p (n e u) -> p n e u", n=2, u=2),
-                turned[:].rearrange("p (n u e) -> p n e u", n=2, u=2),
-            )
-            cols = slice(pair * 2 * P, (pair + 1) * 2 * P)
-            nc.vector.quantize_mx(out=v_words[:, cols].bitcast(FP8X4), scales=v_scales[:, cols], in_=woven[:])
+        cos = [cosine(0, dot_cross0, inv0), cosine(1, dot_cross1, inv1)]
+        exps = [exponentiate(t, cos[t]) for t in range(Q_TILES)]
+        for h in range(2):
+            later = held.tile([P, I], BF16, name=f"picked{2 + h}", tag=f"inv_t1_{h}")
+            picked.append(pick_values(later[:], 2 + h, vector_copy))
 
         def run_sums(p):
             run_sum = work.tile([P, G], F32, name="run_sum")
@@ -233,118 +245,100 @@ def tile_attend_planecos_outside_bymember_kernel(
             )
             return run_sum
 
-        def turn_scaled(t, p):
+        def inverse_outside(t, run_sum, z0, root):
+            nc.scalar.activation(out=root, in_=run_sum[:], func=ACT.Abs_reciprocal_sqrt, scale=-1.0, bias=z0[:])
+            k0_twice = work.tile([P, G, 2], F32, name="k0_twice")
+            nc.scalar.activation(out=k0_twice[:], in_=root.unsqueeze(2).to_broadcast([P, G, 2]), func=ACT.Square)
+            k0_t = bank(6 - t)
+            turn(k0_t[:, 0:P], k0_twice[:].rearrange("p g h -> p (g h)"))
+            return k0_t
+
+        def times_slot_factor(t, p):
             p_t = bank(t)
-            turn_sum(p_t[:], [p[:].rearrange("p j s -> p (j s)")])
-            scaled = work.tile([P, P, PACK], F32, name="scaled")
+            turn(p_t[:], p[:].rearrange("p j s -> p (j s)"))
+            p_os_t = work.tile([P, P, PACK], F32, name="p_os_t")
             nc.vector.tensor_tensor(
-                out=scaled[:],
+                out=p_os_t[:],
                 in0=p_t[:].rearrange("p (j q) -> p q j", j=PACK),
                 in1=os_sb[:].unsqueeze(1).to_broadcast([P, P, PACK]),
                 op=ALU.mult,
             )
-            return scaled
+            return p_os_t
 
-        def inverse_outside(t, run_sum, z0):
-            root = held.tile([P, G], F32, name=f"root{t}", tag=("lam1", "root1")[t], align_bytes=64)
-            nc.scalar.activation(
-                out=root[:], in_=run_sum[:], func=ACT.Abs_reciprocal_sqrt, scale=-1.0, bias=z0[:]
-            )
-            k0_twice = work.tile([P, G, 2], F32, name="k0_twice")
-            nc.scalar.activation(
-                out=k0_twice[:], in_=root[:].unsqueeze(2).to_broadcast([P, G, 2]), func=ACT.Square
-            )
-            k0_t = bank(6 - t)
-            nc.tensor.transpose(k0_t[:, 0:P], k0_twice[:].rearrange("p g h -> p (g h)"), ident[:])
-            return k0_t
+        v_words = held.tile([P, E], U32, name="v_words", align_bytes=MX_ALIGN)
+        v_scales = held.tile([P, E], U8, name="v_scales", align_bytes=MX_ALIGN)
 
-        def weights(scaled, k0_t):
-            w_woven = work.tile([P, P, PACK], BF16, name="w_woven", align_bytes=64)
+        def quantise_values(pair):
+            turned = bank(3 - pair)
+            for n in range(2):
+                slot_words = picked[2 * pair + n].bitcast(F32)
+                for u in range(2):
+                    nc.tensor.transpose(
+                        turned[:, (2 * n + u) * P : (2 * n + u + 1) * P], slot_words[:, u : 2 * P : 2], ident[:]
+                    )
+            woven = work.tile([P, BANK], F32, name="v_woven", align_bytes=MX_ALIGN)
+            vector_copy(
+                woven[:].rearrange("p (n e u) -> p n e u", n=2, u=2),
+                turned[:].rearrange("p (n u e) -> p n e u", n=2, u=2),
+            )
+            cols = slice(pair * 2 * P, (pair + 1) * 2 * P)
+            nc.vector.quantize_mx(
+                out=v_words[:, cols].bitcast(FP8X4), scales=v_scales[:, cols], in_=woven[:].bitcast(BF16)
+            )
+
+        def quantise_weights(t, p_os_t, k0_t):
+            woven = held.tile([P, P, PACK], BF16, name=f"w_woven{t}", tag=f"w_woven{t}", align_bytes=MX_ALIGN)
             nc.vector.tensor_tensor(
-                out=w_woven[:],
-                in0=scaled[:],
+                out=woven[:],
+                in0=p_os_t[:],
                 in1=k0_t[:, 0:P].unsqueeze(2).to_broadcast([P, P, PACK]),
                 op=ALU.mult,
             )
-            w_words = work.tile([P, P], U32, name="w_words", align_bytes=64)
-            w_scales = work.tile([P, P], U8, name="w_scales", align_bytes=64)
+            w_words = work.tile([P, P], U32, name="w_words", align_bytes=MX_ALIGN)
+            w_scales = work.tile([P, P], U8, name="w_scales", align_bytes=MX_ALIGN)
             nc.vector.quantize_mx(
-                out=w_words[:].bitcast(FP8X4), scales=w_scales[:], in_=w_woven[:].rearrange("p q j -> p (q j)")
+                out=w_words[:].bitcast(FP8X4), scales=w_scales[:], in_=woven[:].rearrange("p q j -> p (q j)")
             )
             return w_words, w_scales
 
-        def gather_members():
-            mine = held.tile([P, E_TILES + 1, Q], F32, name="mine", tag="root1", align_bytes=64)
-            scalar_move(mine[:, E_TILES, :], mgain_sb[:].indirect(list3[:]))
-            for c in range(E_TILES):
-                scalar_move(mine[:, c, :], member_sb[c][:].indirect(list3[:]))
-            return mine
+        sums = [run_sums(p) for p, z0 in exps]
+        after_exp = held.tile([P, Q + G], F32, name="after_exp", tag="lam1", align_bytes=MX_ALIGN)
+        gain = after_exp[:, 0:Q]
+        scalar_gather(gain, mgain_sb[:].indirect(list3[:]))
+        root1 = held.tile([P, G], F32, name="root1", tag="root1", align_bytes=MX_ALIGN)
+        roots = (after_exp[:, Q:], root1[:])
+        k0_t = [inverse_outside(t, sums[t], exps[t][1], roots[t]) for t in range(Q_TILES)]
+        p_os_t = [times_slot_factor(t, exps[t][0]) for t in range(Q_TILES)]
+        for pair in range(E_TILES // 2):
+            quantise_values(pair)
+        columns = held.tile([P, E_TILES, Q], F32, name="columns", tag="root1", align_bytes=MX_ALIGN)
+        for c in range(E_TILES):
+            scalar_gather(columns[:, c, :], member_sb[c][:].indirect(list3[:]))
+        weights = [quantise_weights(t, p_os_t[t], k0_t[t]) for t in range(Q_TILES)]
 
-        def read_out(t, w_words, w_scales, mine):
-            cols = slice(t * P, (t + 1) * P)
+        for t, (w_words, w_scales) in enumerate(weights):
+            rows = slice(t * P, (t + 1) * P)
             o = bank(7 - 3 * t)
             for c in range(E_TILES):
-                e_cols = slice(c * P, (c + 1) * P)
+                features = slice(c * P, (c + 1) * P)
                 nc.tensor.matmul_mx(
-                    out=o[:, e_cols],
-                    lhsT=v_words[:, e_cols].bitcast(FP8X4),
-                    lhsT_scale=v_scales[:, e_cols],
+                    out=o[:, features],
+                    lhsT=v_words[:, features].bitcast(FP8X4),
+                    lhsT_scale=v_scales[:, features],
                     rhs=w_words[:].bitcast(FP8X4),
                     rhs_scale=w_scales[:],
                     start=True,
                     stop=True,
                 )
-            gained = work.tile([P, E_TILES, P], F32, name="gained")
+            gained = held.tile(
+                [P, E_TILES, P], F32, name=f"gained{t}", tag=("w_woven1", "gained1")[t], align_bytes=MX_ALIGN
+            )
             nc.vector.tensor_tensor(
                 out=gained[:],
                 in0=o[:].rearrange("p (c q) -> p c q", q=P),
-                in1=mine[:, E_TILES, cols].unsqueeze(1).to_broadcast([P, E_TILES, P]),
+                in1=gain[:, rows].unsqueeze(1).to_broadcast([P, E_TILES, P]),
                 op=ALU.mult,
             )
             y = work.tile([P, E_TILES, P], F32, name="y")
-            nc.vector.tensor_tensor(out=y[:], in0=gained[:], in1=mine[:, 0:E_TILES, cols], op=ALU.add)
-            nc.sync.dma_start(out=out.rearrange("(c p) q -> p c q", p=P)[:, :, cols], in_=y[:])
-
-        a0 = score_plane(0, 0, (scalar_move, vector_copy))
-        b0 = score_plane(1, 0, (scalar_copy,))
-        for k, plane in enumerate((a0, b0)):
-            for n in range(2):
-                look_up(k, 0, n, plane, vector_copy)
-        a1 = score_plane(0, 1, (scalar_copy,))
-        b1 = score_plane(1, 1, (scalar_copy,))
-        turned0 = [products(0, h) for h in range(2)]
-        look_up(0, 1, 0, a1, vector_copy)
-        look_up(0, 1, 1, a1, scalar_move)
-        for n in range(2):
-            look_up(1, 1, n, b1, scalar_move)
-
-        def pick_values(dst, c, gather):
-            gather(dst, vals_sb[c][:].indirect(list1[:]))
-            return dst
-
-        turned1 = [products(1, 0)]
-        den0 = [square(0, h, turned0[h]) for h in range(2)]
-        turned1.append(products(1, 1))
-        picked = [pick_values(squares[0][:, 2, 0:HALF].bitcast(BF16), 0, scalar_move)]
-        inv_len0 = [inverse_length(0, h, den0[h]) for h in range(2)]
-        den1 = [square(1, h, turned1[h]) for h in range(2)]
-        inv_len1 = [inverse_length(1, h, den1[h]) for h in range(2)]
-        pick1 = held.tile([P, I], BF16, name="pick1", tag="points1_1", align_bytes=64)
-        picked.append(pick_values(pick1[:], 1, vector_copy))
-        cos0 = cosine(0, turned0, inv_len0)
-        cos1 = cosine(1, turned1, inv_len1)
-        soft = [exponentiate(0, cos0), exponentiate(1, cos1)]
-        pick2 = held.tile([P, I], BF16, name="pick2", tag="inv_len1_0")
-        picked.append(pick_values(pick2[:], 2, vector_copy))
-        pick3 = held.tile([P, I], BF16, name="pick3", tag="inv_len1_1")
-        picked.append(pick_values(pick3[:], 3, vector_copy))
-        sums = [run_sums(p) for p, z0 in soft]
-        k0_t = [inverse_outside(t, sums[t], soft[t][1]) for t in range(Q_TILES)]
-        scaled = [turn_scaled(t, soft[t][0]) for t in range(Q_TILES)]
-        turn_values(picked, 0, vector_copy)
-        turn_values(picked, 1, scalar_copy)
-        w0 = weights(scaled[0], k0_t[0])
-        w1 = weights(scaled[1], k0_t[1])
-        mine = gather_members()
-        read_out(0, *w0, mine)
-        read_out(1, *w1, mine)
+            nc.vector.tensor_tensor(out=y[:], in0=gained[:], in1=columns[:, :, rows], op=ALU.add)
+            nc.sync.dma_start(out=out.rearrange("(c p) q -> p c q", p=P)[:, :, rows], in_=y[:])

from contextlib import ExitStack

import concourse.mybir as mybir
from concourse.masks import make_identity

D, T, I, Q, E, G, M = 512, 2048, 512, 256, 512, 64, 1024
FLOPS = 2 * (2 * Q * D * T + E * I * Q)

F32 = mybir.dt.float32
BF16 = mybir.dt.bfloat16
I32 = mybir.dt.int32
U32 = mybir.dt.uint32
U16 = mybir.dt.uint16
U8 = mybir.dt.uint8
FP8X4 = mybir.dt.float8_e4m3fn_x4
ACT = mybir.ActivationFunctionType
ALU = mybir.AluOpType
AXIS = mybir.AxisListType

P = 128
PACK = 4
BANK = 512
QUADRANT = 32
SCALE_ROWS = 4
LIST_ROWS = 16
MX_ALIGN = 64
Q_TILES = Q // P
E_TILES = E // P
KEY_CHUNKS = T // BANK
HALF = I // 2


def tile_attend_planecos_outside_bymember_kernel(
    tc, query, query2, keys_words, keys_scales, lam, slot_factor, vals, member, mgain, offs, offs2, offs3, out
):
    nc = tc.nc
    with ExitStack() as ctx:
        held = ctx.enter_context(tc.tile_pool(name="held", bufs=1))
        work = ctx.enter_context(tc.tile_pool(name="work", bufs=2))
        psum = ctx.enter_context(tc.psum_pool(name="psum", bufs=1))

        def bank(n):
            return psum.tile([P, BANK], F32, name=f"bank{n}", tag=f"bank{n}")

        def vector_copy(dst, src):
            nc.vector.tensor_copy(out=dst, in_=src)

        def scalar_copy(dst, src):
            nc.scalar.copy(out=dst, in_=src)

        def scalar_gather(dst, src):
            nc.scalar.activation(out=dst, in_=src, func=ACT.Copy)

        key_scales = held.tile([P, BANK], U8, name="key_scales", align_bytes=MX_ALIGN)
        nc.gpsimd.memset(key_scales[:].bitcast(U32), 0)
        for quad in range(P // QUADRANT):
            scale_rows = keys_scales[0, SCALE_ROWS * quad : SCALE_ROWS * (quad + 1), :]
            nc.sync.dma_start(
                out=key_scales[QUADRANT * quad : QUADRANT * quad + SCALE_ROWS * KEY_CHUNKS, :].bitcast(I32),
                in_=scale_rows.rearrange("r (n c) -> n r c", n=KEY_CHUNKS).bitcast(I32),
            )
        words_hbm = keys_words[0].rearrange("p n t -> p (n t)").bitcast(I32)
        raw_q = [held.tile([P, PACK, Q], F32, name=f"raw_q{k}") for k in range(2)]
        key_words = [
            held.tile([P, BANK], U32, name=f"key_words{n}", align_bytes=MX_ALIGN) for n in range(KEY_CHUNKS)
        ]

        def load_query(k):
            nc.sync.dma_start(out=raw_q[k][:], in_=(query, query2)[k].rearrange("(p j) w -> p j w", j=PACK))

        load_query(0)
        for n in range(KEY_CHUNKS):
            nc.sync.dma_start(out=key_words[n][:].bitcast(I32), in_=words_hbm[:, n * BANK : (n + 1) * BANK])
        load_query(1)
        list1 = held.tile([P, I // LIST_ROWS], U16, name="list1")
        list2 = held.tile([P, I // LIST_ROWS], U16, name="list2")
        list3 = held.tile([P, Q // LIST_ROWS], U16, name="list3")
        nc.sync.dma_start(list1[:], offs)
        nc.sync.dma_start(list2[:], offs2)
        vals_sb = [held.tile([P, T], F32, name=f"vals{c}") for c in range(E_TILES)]
        for c in range(E_TILES):
            nc.sync.dma_start(out=vals_sb[c][:], in_=vals[c * P : (c + 1) * P, :])
        nc.sync.dma_start(list3[:], offs3)
        lam_sb = [
            held.tile([P, 1], F32, name=f"lam{t}", tag=f"lam{t}", align_bytes=MX_ALIGN) for t in range(Q_TILES)
        ]
        for t in range(Q_TILES):
            nc.sync.dma_start(out=lam_sb[t][:], in_=lam[t * P : (t + 1) * P, :])
        os_sb = held.tile([P, PACK], F32, name="os_sb")
        nc.sync.dma_start(out=os_sb[:], in_=slot_factor.rearrange("o (p j) -> (o p) j", j=PACK))
        mgain_sb = held.tile([P, M], F32, name="mgain_sb")
        nc.sync.dma_start(out=mgain_sb[:], in_=mgain)
        member_sb = [held.tile([P, M], F32, name=f"member{c}") for c in range(E_TILES)]
        for c in range(E_TILES):
            nc.sync.dma_start(out=member_sb[c][:], in_=member[c * P : (c + 1) * P, :])

        ident = held.tile([P, P], F32, name="ident")
        make_identity(nc, ident[:])
        one_half = held.tile([P, 1], F32, name="one_half", tag="one_half")
        nc.gpsimd.memset(one_half[:], 0.5)

        warm = held.tile([P, 1], F32, name="warm")
        nc.scalar.activation(out=warm[:], in_=one_half[:], func=ACT.Abs_reciprocal_sqrt)

        def quantise_query(k, t):
            tag = "points0_0_0" if (k, t) == (1, Q_TILES - 1) else f"q_woven{k}_{t}"
            woven = held.tile([P, P, PACK], BF16, name=f"q_woven{k}_{t}", tag=tag, align_bytes=MX_ALIGN)
            vector_copy(
                woven[:].rearrange("p (c i) j -> p c j i", i=4),
                raw_q[k][:, :, t * P : (t + 1) * P].rearrange("p j (c i) -> p c j i", i=4),
            )
            words = held.tile([P, P], U32, name=f"q_words{k}_{t}", align_bytes=MX_ALIGN)
            scales = held.tile([P, P], U8, name=f"q_scales{k}_{t}", align_bytes=MX_ALIGN)
            nc.vector.quantize_mx(
                out=words[:].bitcast(FP8X4), scales=scales[:], in_=woven[:].rearrange("p w j -> p (w j)")
            )
            return words, scales

        quantised = {(k, t): quantise_query(k, t) for k in range(2) for t in range(Q_TILES)}

        def score_plane(k, t):
            plane = held.tile([P, T], F32, name=f"plane{k}_{t}", tag=f"plane{k}_{t}")
            q_words, q_scales = quantised[k, t]
            for n in range(KEY_CHUNKS):
                acc = bank(t * KEY_CHUNKS + n)
                nc.tensor.matmul_mx(
                    out=acc[:],
                    lhsT=q_words[:].bitcast(FP8X4),
                    lhsT_scale=q_scales[:],
                    rhs=key_words[n][:].bitcast(FP8X4),
                    rhs_scale=key_scales[SCALE_ROWS * n : P, :],
                    start=True,
                    stop=True,
                )
                empty = vector_copy if (k, t, n) == (0, 0, 1) else scalar_copy
                empty(plane[:, n * BANK : (n + 1) * BANK], acc[:])
            return plane

        planes = {(k, t): score_plane(k, t) for k in range(2) for t in range(Q_TILES)}

        points = {}

        def look_up(k, t, n, gather):
            name = f"points{k}_{t}_{n}"
            points[k, t, n] = held.tile([P, I], F32, name=name, tag=name, align_bytes=MX_ALIGN)
            gather(points[k, t, n][:], planes[k, t][:].indirect((list1, list2)[n][:]))

        for k, t, n in ((0, 0, 0), (0, 0, 1), (0, 1, 0), (1, 0, 0), (1, 0, 1)):
            look_up(k, t, n, vector_copy)
        for k, t, n in ((0, 1, 1), (1, 1, 0), (1, 1, 1)):
            look_up(k, t, n, scalar_gather)

        def products(t, h, parts):
            slots = slice(h * HALF, (h + 1) * HALF)
            a1, a2, b1, b2 = (points[k, t, n][:, slots] for k in range(2) for n in range(2))
            nc.vector.tensor_tensor(out=parts[:, 0, :], in0=a1, in1=a2, op=ALU.mult)
            nc.vector.tensor_tensor(out=parts[:, 1, :], in0=b1, in1=b2, op=ALU.mult)
            nc.vector.tensor_tensor(out=parts[:, 2, :], in0=a1, in1=b2, op=ALU.mult)
            nc.vector.scalar_tensor_tensor(
                out=parts[:, 3, :], in0=b1, scalar=-1.0, in1=a2, op0=ALU.mult, op1=ALU.mult
            )
            dot_cross_t = bank(7 - 2 * t - h)
            passes = [(n, b) for n in (0, 3, 1, 2) for b in range(HALF // P)]
            for n, b in passes:
                at = (n // 2) * HALF + b * P
                nc.tensor.matmul(
                    out=dot_cross_t[:, at : at + P],
                    lhsT=parts[:, n, b * P : (b + 1) * P],
                    rhs=ident[:],
                    is_transpose=True,
                    start=((n, b) == passes[0]),
                    stop=((n, b) == passes[-1]),
                )
            return dot_cross_t

        def squared_lengths(dot_cross_t, squares, lalb_t):
            nc.scalar.activation(out=squares, in_=dot_cross_t[:], func=ACT.Square)
            nc.vector.tensor_tensor(out=lalb_t, in0=squares[:, 0:HALF], in1=squares[:, HALF:I], op=ALU.add)

        def inverse_root(t, h, lalb_t):
            inv_t = held.tile([P, HALF], F32, name=f"inv_t{t}_{h}", tag=f"inv_t{t}_{h}")
            nc.scalar.activation(out=inv_t[:], in_=lalb_t, func=ACT.Abs_reciprocal_sqrt, bias=one_half[:])
            return inv_t

        def pick_values(dst, c, gather):
            gather(dst, vals_sb[c][:].indirect(list1[:]))
            return dst

        def halves(tile):
            return [tile[:, h * HALF : (h + 1) * HALF] for h in range(2)]

        parts0 = held.tile([P, 2, 4, HALF], F32, name="parts0", tag="plane1_0")
        dot_cross0 = [products(0, h, parts0[:, h]) for h in range(2)]
        after_b1 = held.tile([P, 3, I], F32, name="after_b1", tag="plane1_1")
        squares1 = held.tile([P, 2, I], F32, name="squares1", tag="plane1_0")
        parts1 = held.tile([P, 2, 4, HALF], F32, name="parts1")
        dot_cross1 = [products(1, 0, parts1[:, 0])]
        lalb0 = halves(held.tile([P, I], F32, name="lalb0"))
        for h in range(2):
            squared_lengths(dot_cross0[h], after_b1[:, h, :], lalb0[h])
        dot_cross1.append(products(1, 1, parts1[:, 1]))
        picked = [pick_values(after_b1[:, 2, 0:HALF].bitcast(BF16), 0, scalar_gather)]
        inv0 = [inverse_root(0, h, lalb0[h]) for h in range(2)]
        lalb1 = halves(held.tile([P, I], F32, name="lalb1"))
        for h in range(2):
            squared_lengths(dot_cross1[h], squares1[:, h, :], lalb1[h])
        inv1 = [inverse_root(1, h, lalb1[h]) for h in range(2)]
        picked1 = held.tile([P, I], BF16, name="picked1", tag="points1_1_1", align_bytes=MX_ALIGN)
        picked.append(pick_values(picked1[:], 1, vector_copy))

        def turn(dst, src):
            for b in range(dst.shape[1] // P):
                nc.tensor.transpose(dst[:, b * P : (b + 1) * P], src[:, b * P : (b + 1) * P], ident[:])

        def cosine(t, dot_cross_t, inv_t):
            cos_t = held.tile([P, I], F32, name=f"cos_t{t}", tag=f"points0_{1 - t}_0", align_bytes=MX_ALIGN)
            cos = bank(3 - t)
            for h, (src, dst) in enumerate(zip(halves(cos_t), halves(cos))):
                nc.vector.tensor_tensor(out=src, in0=dot_cross_t[h][:, 0:HALF], in1=inv_t[h][:], op=ALU.mult)
                turn(dst, src)
            return cos

        def exponentiate(t, cos):
            p = work.tile([P, PACK, P], F32, name="p")
            z0 = held.tile([P, 1], F32, name=f"z0_{t}", tag=("one_half", "z0_1")[t])
            nc.scalar.activation(
                out=p[:],
                in_=cos[:].rearrange("p (s j) -> p j s", j=PACK),
                func=ACT.Exp,
                scale=lam_sb[t][:],
                accum_out=z0[:],
            )
            return p, z0

        cos = [cosine(0, dot_cross0, inv0), cosine(1, dot_cross1, inv1)]
        exps = [exponentiate(t, cos[t]) for t in range(Q_TILES)]
        for h in range(2):
            later = held.tile([P, I], BF16, name=f"picked{2 + h}", tag=f"inv_t1_{h}")
            picked.append(pick_values(later[:], 2 + h, vector_copy))

        def run_sums(p):
            run_sum = work.tile([P, G], F32, name="run_sum")
            nc.vector.tensor_reduce(
                out=run_sum[:], in_=p[:].rearrange("p j (g h) -> p g j h", h=2), axis=AXIS.XY, op=ALU.add
            )
            return run_sum

        def inverse_outside(t, run_sum, z0, root):
            nc.scalar.activation(out=root, in_=run_sum[:], func=ACT.Abs_reciprocal_sqrt, scale=-1.0, bias=z0[:])
            k0_twice = work.tile([P, G, 2], F32, name="k0_twice")
            nc.scalar.activation(out=k0_twice[:], in_=root.unsqueeze(2).to_broadcast([P, G, 2]), func=ACT.Square)
            k0_t = bank(6 - t)
            turn(k0_t[:, 0:P], k0_twice[:].rearrange("p g h -> p (g h)"))
            return k0_t

        def times_slot_factor(t, p):
            p_t = bank(t)
            turn(p_t[:], p[:].rearrange("p j s -> p (j s)"))
            p_os_t = work.tile([P, P, PACK], F32, name="p_os_t")
            nc.vector.tensor_tensor(
                out=p_os_t[:],
                in0=p_t[:].rearrange("p (j q) -> p q j", j=PACK),
                in1=os_sb[:].unsqueeze(1).to_broadcast([P, P, PACK]),
                op=ALU.mult,
            )
            return p_os_t

        v_words = held.tile([P, E], U32, name="v_words", align_bytes=MX_ALIGN)
        v_scales = held.tile([P, E], U8, name="v_scales", align_bytes=MX_ALIGN)

        def quantise_values(pair):
            turned = bank(3 - pair)
            for n in range(2):
                slot_words = picked[2 * pair + n].bitcast(F32)
                for u in range(2):
                    nc.tensor.transpose(
                        turned[:, (2 * n + u) * P : (2 * n + u + 1) * P], slot_words[:, u : 2 * P : 2], ident[:]
                    )
            woven = work.tile([P, BANK], F32, name="v_woven", align_bytes=MX_ALIGN)
            vector_copy(
                woven[:].rearrange("p (n e u) -> p n e u", n=2, u=2),
                turned[:].rearrange("p (n u e) -> p n e u", n=2, u=2),
            )
            cols = slice(pair * 2 * P, (pair + 1) * 2 * P)
            nc.vector.quantize_mx(
                out=v_words[:, cols].bitcast(FP8X4), scales=v_scales[:, cols], in_=woven[:].bitcast(BF16)
            )

        def quantise_weights(t, p_os_t, k0_t):
            woven = held.tile([P, P, PACK], BF16, name=f"w_woven{t}", tag=f"w_woven{t}", align_bytes=MX_ALIGN)
            nc.vector.tensor_tensor(
                out=woven[:],
                in0=p_os_t[:],
                in1=k0_t[:, 0:P].unsqueeze(2).to_broadcast([P, P, PACK]),
                op=ALU.mult,
            )
            w_words = work.tile([P, P], U32, name="w_words", align_bytes=MX_ALIGN)
            w_scales = work.tile([P, P], U8, name="w_scales", align_bytes=MX_ALIGN)
            nc.vector.quantize_mx(
                out=w_words[:].bitcast(FP8X4), scales=w_scales[:], in_=woven[:].rearrange("p q j -> p (q j)")
            )
            return w_words, w_scales

        sums = [run_sums(p) for p, z0 in exps]
        after_exp = held.tile([P, Q + G], F32, name="after_exp", tag="lam1", align_bytes=MX_ALIGN)
        gain = after_exp[:, 0:Q]
        scalar_gather(gain, mgain_sb[:].indirect(list3[:]))
        root1 = held.tile([P, G], F32, name="root1", tag="root1", align_bytes=MX_ALIGN)
        roots = (after_exp[:, Q:], root1[:])
        k0_t = [inverse_outside(t, sums[t], exps[t][1], roots[t]) for t in range(Q_TILES)]
        p_os_t = [times_slot_factor(t, exps[t][0]) for t in range(Q_TILES)]
        for pair in range(E_TILES // 2):
            quantise_values(pair)
        columns = held.tile([P, E_TILES, Q], F32, name="columns", tag="root1", align_bytes=MX_ALIGN)
        for c in range(E_TILES):
            scalar_gather(columns[:, c, :], member_sb[c][:].indirect(list3[:]))
        weights = [quantise_weights(t, p_os_t[t], k0_t[t]) for t in range(Q_TILES)]

        for t, (w_words, w_scales) in enumerate(weights):
            rows = slice(t * P, (t + 1) * P)
            o = bank(7 - 3 * t)
            for c in range(E_TILES):
                features = slice(c * P, (c + 1) * P)
                nc.tensor.matmul_mx(
                    out=o[:, features],
                    lhsT=v_words[:, features].bitcast(FP8X4),
                    lhsT_scale=v_scales[:, features],
                    rhs=w_words[:].bitcast(FP8X4),
                    rhs_scale=w_scales[:],
                    start=True,
                    stop=True,
                )
            gained = held.tile(
                [P, E_TILES, P], F32, name=f"gained{t}", tag=("w_woven1", "gained1")[t], align_bytes=MX_ALIGN
            )
            nc.vector.tensor_tensor(
                out=gained[:],
                in0=o[:].rearrange("p (c q) -> p c q", q=P),
                in1=gain[:, rows].unsqueeze(1).to_broadcast([P, E_TILES, P]),
                op=ALU.mult,
            )
            y = work.tile([P, E_TILES, P], F32, name="y")
            nc.vector.tensor_tensor(out=y[:], in0=gained[:], in1=columns[:, :, rows], op=ALU.add)
            nc.sync.dma_start(out=out.rearrange("(c p) q -> p c q", p=P)[:, :, rows], in_=y[:])
